import numpy as np
import ml_dtypes


def mxq(x, axis, fmt="e4m3"):
    dtype, down = {"e4m3": (ml_dtypes.float8_e4m3fn, 7), "e5m2": (ml_dtypes.float8_e5m2, 14)}[fmt]
    v = np.moveaxis(np.asarray(x, np.float32).astype(ml_dtypes.bfloat16).astype(np.float64), axis, -1)
    blocks = v.reshape(v.shape[:-1] + (-1, 32))
    amax = np.abs(blocks).max(-1, keepdims=True)
    byte = np.maximum(np.where(amax > 0, np.frexp(amax)[1] - 1 + 127, 0) - down, 1)
    scale = np.exp2(byte - 127.0)
    codes = (blocks / scale).astype(np.float32).astype(dtype).astype(np.float64)
    return np.moveaxis((codes * scale).reshape(v.shape), -1, axis)


WIDE = False


def mx_kscale(k):
    if not WIDE:
        return np.ones(k)
    levels = np.array([10, -10, 5, -5, 0])
    if k % 512:
        return np.exp2(np.random.permutation(np.resize(levels, k // 32))).repeat(32)
    a = np.empty((k // 512, 16))
    for p in range(k // 512):
        a[p, :8] = np.random.permutation(np.resize(levels, 8))
        for g in range(8):
            far = levels[np.abs(levels - a[p, g]) >= 10]
            a[p, g + 8] = far[np.random.randint(len(far))]
    return np.exp2(a.ravel()).repeat(32)


def f64(x):
    return np.asarray(x).astype(np.float64)


def striped(idx):
    return np.tile(np.asarray(idx).reshape(-1, 16).T, (8, 1)).astype(np.uint16)


def unstriped(offs):
    return offs[:16].T.reshape(-1).astype(np.int64)


E2M1 = np.array([0.0, 0.5, 1.0, 1.5, 2.0, 3.0, 4.0, 6.0, -0.0, -0.5, -1.0, -1.5, -2.0, -3.0, -4.0, -6.0])


def pack_weight(w, fmt):
    k, n = w.shape
    w = f64(np.asarray(w, np.float32).astype(ml_dtypes.bfloat16)).reshape(k // 32, 32, n)
    amax = np.abs(w).max(1)
    if fmt == "e4m3":
        byte = np.frexp(amax)[1] - 1 + 127 - 7
    else:
        mant, ex = np.frexp(amax / 6.0)
        byte = np.where(mant > 0.5, ex, ex - 1) + 127
    byte = np.clip(np.where(amax > 0, byte, 1), 1, 254)
    scaled = (w * np.exp2(127.0 - byte)[:, None, :]).reshape(k, n).astype(np.float32)
    by_word = np.ascontiguousarray(scaled.reshape(k // 512, 128, 4, n).transpose(0, 1, 3, 2))
    if fmt == "e4m3":
        words = by_word.astype(ml_dtypes.float8_e4m3fn).view(np.uint8)
    else:
        c = by_word.astype(ml_dtypes.float4_e2m1fn).view(np.uint8) & 0xF
        words = (c[..., 0::2] | (c[..., 1::2] << 4)).reshape(k // 512, 128, 2 * n)
    return np.ascontiguousarray(words), np.ascontiguousarray(byte.astype(np.uint8).reshape(k // 512, 16, n))


def unpack_weight(words, scales, fmt):
    g, _, n = scales.shape
    words = np.ascontiguousarray(words).reshape(g, 128, n, -1)
    if fmt == "e4m3":
        vals = words.view(ml_dtypes.float8_e4m3fn).astype(np.float64)
    else:
        nib = np.empty((g, 128, n, 4), np.uint8)
        nib[..., 0::2] = words & 0xF
        nib[..., 1::2] = words >> 4
        vals = E2M1[nib]
    vals = vals * np.repeat(np.exp2(scales.astype(np.float64) - 127.0), 8, axis=1)[..., None]
    return vals.transpose(0, 1, 3, 2).reshape(g * 512, n)


def softplus(v):
    return np.log(1.0 + np.exp(v))


def sigmoid(v):
    return 1.0 / (1.0 + np.exp(-v))


K, R, F, T, J, G = 512, 128, 512, 2048, 512, 128


def setup_inputs():
    n = np.random.standard_normal
    idx = np.random.permutation(T)[:J]
    fk = mx_kscale(K)
    ff = mx_kscale(F)
    tabp = pack_weight(n((K, T)) / fk[:, None], "e2m1")
    return {
        "tab_words": tabp[0],
        "tab_scales": tabp[1],
        "w1": (n((K, R)) * 1 / np.sqrt(K) * fk[:, None]).astype(np.float32),
        "floor": (np.random.uniform(0.2, 0.8, (R, 1))).astype(np.float32),
        "wo": (n((F, R)) * 1 / np.sqrt(F) * ff[:, None]).astype(np.float32),
        "dy": (n((F, G)) / ff[:, None]).astype(np.float32),
        "old": (0.5 * n((R, J))).astype(np.float32),
        "offs": striped(idx),
    }


def reference(tab_words, tab_scales, w1, floor, wo, dy, old, offs):
    idx = unstriped(offs)
    tabu = unpack_weight(tab_words, tab_scales, "e2m1")
    w1q = mxq(f64(w1), 0, "e4m3")
    tabidxg = tabu[:, idx]
    a = w1q.T @ tabidxg
    h0 = softplus(a)
    h1 = np.log(h0 + f64(floor))
    m1 = h1.reshape(R, G, J // G).mean(axis=2)
    u1 = np.tanh(np.exp(m1))
    woq = mxq(f64(wo), 0, "e4m3")
    dyq = mxq(f64(dy), 0, "e4m3")
    c0 = woq.T @ dyq
    dm1 = c0 * (1.0 - np.square(u1)) * np.exp(m1)
    e1 = dm1 / 4.0
    r1 = np.repeat(e1, J // G, axis=1)
    dh0 = r1 / (h0 + f64(floor))
    da = dh0 * sigmoid(a)
    y = da + f64(old)
    return y

@@ -1,0 +1,171 @@
+from contextlib import ExitStack
+
+import concourse.mybir as mybir
+
+K, R, F, T, J, G = 512, 128, 512, 2048, 512, 128
+FLOPS = 2 * K * R * J + 2 * F * R * G
+
+F32 = mybir.dt.float32
+BF16 = mybir.dt.bfloat16
+I32 = mybir.dt.int32
+U32 = mybir.dt.uint32
+U16 = mybir.dt.uint16
+U8 = mybir.dt.uint8
+FP8X4 = mybir.dt.float8_e4m3fn_x4
+FP4X4 = mybir.dt.float4_e2m1fn_x4
+ACT = mybir.ActivationFunctionType
+ALU = mybir.AluOpType
+AX = mybir.AxisListType
+
+P = 128
+PACK = 4
+POOL = J // G
+HALVES = 2
+JH = J // HALVES
+GH = G // HALVES
+QUARTERS = 4
+JQ = J // QUARTERS
+
+
+def tile_attend_cgeometricpool_kernel(tc, tab_words, tab_scales, w1, floor, wo, dy, old, offs, out):
+    nc = tc.nc
+    with ExitStack() as ctx:
+        sb = ctx.enter_context(tc.tile_pool(name="sb", bufs=1))
+        ps = ctx.enter_context(tc.psum_pool(name="ps", bufs=1))
+
+        offsets = sb.tile([P, J // 16], U16, name="offsets")
+        words = sb.tile([P, T], U16, name="words", tag="words_then_dy", align_bytes=64)
+        planes = sb.tile([P, T], U8, name="planes", align_bytes=64)
+        w1_raw = sb.tile([P, PACK, R], F32, name="w1_raw", tag="weights_raw", align_bytes=64)
+        floor_sb = sb.tile([P, 1], F32, name="floor_sb")
+        half = sb.tile([P, 1], F32, name="half")
+
+        nc.vector.memset(planes[:].bitcast(I32), 0)
+        nc.gpsimd.memset(half[:], 0.5)
+        nc.sync.dma_start(out=words[:].bitcast(I32), in_=tab_words[0].bitcast(I32))
+        nc.sync.dma_start(offsets[:], offs)
+        nc.sync.dma_start(out=w1_raw[:], in_=w1.rearrange("(p j) w -> p j w", j=PACK))
+        nc.sync.dma_start(out=floor_sb[:], in_=floor)
+        for q in range(4):
+            nc.scalar.dma_start(out=planes[32 * q : 32 * q + 4, :].bitcast(I32), in_=tab_scales[0, 4 * q : 4 * q + 4, :].bitcast(I32))
+
+        g_words = sb.tile([P, J], U16, name="g_words", align_bytes=64)
+        nc.vector.tensor_copy(g_words[:], words[:].indirect(offsets[:]))
+
+        w1_bf = sb.tile([P, R, PACK], BF16, name="w1_bf", tag="w1_bf_then_old", align_bytes=64)
+        nc.scalar.copy(out=w1_bf[:], in_=w1_raw[:].rearrange("p j w -> p w j"))
+        w1_codes = sb.tile([P, R], U32, name="w1_codes", align_bytes=64)
+        w1_scales = sb.tile([P, R], U8, name="w1_scales", align_bytes=64)
+
+        g_planes = [sb.tile([P, JH], U8, name="g_planes0", align_bytes=64)]
+        nc.vector.tensor_copy(g_planes[0][:], planes[:].indirect(offsets[:, : JH // 16]))
+        nc.vector.quantize_mx(out=w1_codes[:].bitcast(FP8X4), scales=w1_scales[:], in_=w1_bf[:].rearrange("p w j -> p (w j)"))
+        g_planes.append(sb.tile([P, JH], U8, name="g_planes1", tag="w1_bf_then_old", align_bytes=64))
+        nc.vector.tensor_copy(g_planes[1][:], planes[:].indirect(offsets[:, JH // 16 :]))
+
+        a = [ps.tile([P, JQ], F32, name="a%d" % q) for q in range(QUARTERS)]
+        u = [
+            sb.tile([P, JH], F32, name="u0", tag="pair_then_h0", align_bytes=64),
+            sb.tile([P, JH], F32, name="u1", align_bytes=64),
+        ]
+        absu = sb.tile([P, J], F32, name="absu")
+        quarter = [slice(q * JQ, (q + 1) * JQ) for q in range(QUARTERS)]
+        for q in range(QUARTERS):
+            nc.tensor.matmul_mx(
+                out=a[q][:],
+                lhsT=w1_codes[:].bitcast(FP8X4),
+                lhsT_scale=w1_scales[:],
+                rhs=g_words[:, quarter[q]].bitcast(FP4X4),
+                rhs_scale=g_planes[q // 2][:, (q % 2) * JQ : (q % 2 + 1) * JQ],
+                start=True,
+                stop=True,
+            )
+            nc.scalar.activation(out=u[q // 2][:, quarter[q % 2]], in_=a[q][:], func=ACT.Tanh, scale=0.5)
+
+        wo_raw = sb.tile([P, PACK, R], F32, name="wo_raw", tag="weights_raw", align_bytes=64)
+        dy_raw = sb.tile([P, PACK, G], F32, name="dy_raw", tag="words_then_dy", align_bytes=64)
+        old_sb = sb.tile([P, J], F32, name="old_sb", tag="w1_bf_then_old", align_bytes=64)
+        nc.sync.dma_start(out=wo_raw[:], in_=wo.rearrange("(p j) w -> p j w", j=PACK))
+        nc.sync.dma_start(out=dy_raw[:], in_=dy.rearrange("(p j) w -> p j w", j=PACK))
+        nc.sync.dma_start(out=old_sb[:], in_=old)
+
+        halves = [slice(h * JH, (h + 1) * JH) for h in range(HALVES)]
+        groups = [slice(h * GH, (h + 1) * GH) for h in range(HALVES)]
+        for h, cols in enumerate(halves):
+            nc.vector.scalar_tensor_tensor(out=absu[:, cols], in0=u[h][:], scalar=-1.0, in1=u[h][:], op0=ALU.mult, op1=ALU.max)
+        pair_bf = sb.tile([P, 2, R, PACK], BF16, name="pair_bf", tag="pair_then_h0", align_bytes=64)
+        nc.vector.tensor_copy(out=pair_bf[:, 0], in_=wo_raw[:].rearrange("p j w -> p w j"))
+        nc.vector.tensor_copy(out=pair_bf[:, 1], in_=dy_raw[:].rearrange("p j w -> p w j"))
+        pair_codes = sb.tile([P, 2 * R], U32, name="pair_codes", align_bytes=64)
+        pair_scales = sb.tile([P, 2 * R], U8, name="pair_scales", align_bytes=64)
+        nc.vector.quantize_mx(
+            out=pair_codes[:].bitcast(FP8X4), scales=pair_scales[:], in_=pair_bf[:].rearrange("p s w j -> p (s w j)")
+        )
+        c0 = ps.tile([P, G], F32, name="c0")
+        nc.tensor.matmul_mx(
+            out=c0[:],
+            lhsT=pair_codes[:, :R].bitcast(FP8X4),
+            lhsT_scale=pair_scales[:, :R],
+            rhs=pair_codes[:, R:].bitcast(FP8X4),
+            rhs_scale=pair_scales[:, R:],
+            start=True,
+            stop=True,
+        )
+
+        lsig = sb.tile([P, J], F32, name="lsig")
+        for cols in quarter:
+            nc.scalar.activation(out=lsig[:, cols], in_=absu[:, cols], func=ACT.Ln, bias=half[:], scale=0.5)
+
+        h0 = sb.tile([P, J], F32, name="h0", tag="pair_then_h0", align_bytes=64)
+        h1 = sb.tile([P, J], F32, name="h1")
+        y = sb.tile([P, J], F32, name="y")
+        for q, cols in enumerate(quarter):
+            nc.vector.scalar_tensor_tensor(out=h0[:, cols], in0=a[q][:], scalar=0.0, in1=lsig[:, cols], op0=ALU.max, op1=ALU.subtract)
+        for cols in quarter:
+            nc.scalar.activation(out=h1[:, cols], in_=h0[:, cols], func=ACT.Ln, bias=floor_sb[:], scale=1.0)
+        for q, cols in enumerate(quarter):
+            nc.vector.tensor_tensor(out=y[:, cols], in0=a[q][:], in1=h0[:, cols], op=ALU.subtract)
+        sums = sb.tile([P, G], F32, name="sums")
+        z = sb.tile([P, J], F32, name="z")
+        for h in range(HALVES):
+            nc.vector.tensor_reduce(
+                out=sums[:, groups[h]], in_=h1[:, halves[h]].rearrange("p (g i) -> p g i", i=POOL), axis=AX.X, op=ALU.add
+            )
+        for cols in halves:
+            nc.vector.tensor_tensor(out=z[:, cols], in0=y[:, cols], in1=h1[:, cols], op=ALU.subtract)
+
+        gm = sb.tile([P, G], F32, name="gm", tag="gm_then_w")
+        u1 = sb.tile([P, G], F32, name="tanh_gm")
+        for grp in groups:
+            nc.scalar.activation(out=gm[:, grp], in_=sums[:, grp], func=ACT.Exp, scale=1.0 / POOL)
+        for grp in groups:
+            nc.scalar.activation(out=u1[:, grp], in_=gm[:, grp], func=ACT.Tanh)
+
+        cg = sb.tile([P, G], F32, name="cg")
+        u2 = sb.tile([P, G], F32, name="u2")
+        e1 = sb.tile([P, G], F32, name="e1")
+        nc.vector.scalar_tensor_tensor(out=cg[:], in0=c0[:], scalar=-1.0 / POOL, in1=gm[:], op0=ALU.mult, op1=ALU.mult)
+        w = sb.tile([P, J], F32, name="w", tag="gm_then_w")
+        for cols in halves:
+            nc.scalar.activation(out=w[:, cols], in_=z[:, cols], func=ACT.Exp)
+        for grp in groups:
+            nc.vector.tensor_tensor(out=u2[:, grp], in0=u1[:, grp], in1=u1[:, grp], op=ALU.mult)
+        for grp in groups:
+            nc.vector.scalar_tensor_tensor(out=e1[:, grp], in0=u2[:, grp], scalar=1.0, in1=cg[:, grp], op0=ALU.subtract, op1=ALU.mult)
+
+        da = sb.tile([P, G, POOL], F32, name="da")
+        res = sb.tile([P, J], F32, name="res")
+        for h in range(HALVES):
+            nc.vector.tensor_tensor(
+                out=da[:, groups[h], :],
+                in0=w[:, halves[h]].rearrange("p (g i) -> p g i", i=POOL),
+                in1=e1[:, groups[h]].unsqueeze(2).to_broadcast([P, GH, POOL]),
+                op=ALU.mult,
+            )
+        for h in range(HALVES):
+            cols = halves[h]
+            nc.vector.tensor_tensor(
+                out=res[:, cols], in0=da[:, groups[h], :].rearrange("p g i -> p (g i)"), in1=old_sb[:, cols], op=ALU.add
+            )
+            queue = nc.sync if h == 0 else nc.scalar
+            queue.dma_start(out=out[:, cols], in_=res[:, cols])

@@ -34,34 +34,32 @@ def tile_attend_cgeometricpool_kernel(tc, tab_words, tab_scales, w1, floor, wo, 
         ps = ctx.enter_context(tc.psum_pool(name="ps", bufs=1))
 
         offsets = sb.tile([P, J // 16], U16, name="offsets")
-        words = sb.tile([P, T], U16, name="words", tag="words_then_dy", align_bytes=64)
-        planes = sb.tile([P, T], U8, name="planes", align_bytes=64)
-        w1_raw = sb.tile([P, PACK, R], F32, name="w1_raw", tag="weights_raw", align_bytes=64)
-        floor_sb = sb.tile([P, 1], F32, name="floor_sb")
+        planes = sb.tile([P, T], U8, name="planes", tag="planes_then_dy", align_bytes=64)
+        w1_raw = sb.tile([P, PACK, R], F32, name="w1_raw", tag="w1_raw_then_wo", align_bytes=64)
+        one = sb.tile([P, 1], F32, name="one", tag="words_then_old", align_bytes=64)
         half = sb.tile([P, 1], F32, name="half")
 
+        nc.vector.memset(one[:], 1.0)
         nc.vector.memset(planes[:].bitcast(I32), 0)
-        nc.gpsimd.memset(half[:], 0.5)
-        nc.sync.dma_start(out=words[:].bitcast(I32), in_=tab_words[0].bitcast(I32))
-        nc.sync.dma_start(offsets[:], offs)
+        nc.vector.tensor_scalar_mul(out=half[:], in0=one[:], scalar1=0.5)
         nc.sync.dma_start(out=w1_raw[:], in_=w1.rearrange("(p j) w -> p j w", j=PACK))
-        nc.sync.dma_start(out=floor_sb[:], in_=floor)
+        nc.sync.dma_start(offsets[:], offs)
         for q in range(4):
-            nc.scalar.dma_start(out=planes[32 * q : 32 * q + 4, :].bitcast(I32), in_=tab_scales[0, 4 * q : 4 * q + 4, :].bitcast(I32))
+            nc.sync.dma_start(out=planes[32 * q : 32 * q + 4, :].bitcast(I32), in_=tab_scales[0, 4 * q : 4 * q + 4, :].bitcast(I32))
+        words = sb.tile([P, T], U16, name="words", tag="words_then_old", align_bytes=64)
+        nc.sync.dma_start(out=words[:].bitcast(I32), in_=tab_words[0].bitcast(I32))
 
-        g_words = sb.tile([P, J], U16, name="g_words", align_bytes=64)
-        nc.vector.tensor_copy(g_words[:], words[:].indirect(offsets[:]))
-
-        w1_bf = sb.tile([P, R, PACK], BF16, name="w1_bf", tag="w1_bf_then_old", align_bytes=64)
+        w1_bf = sb.tile([P, R, PACK], BF16, name="w1_bf", tag="w1_bf_then_floor", align_bytes=64)
         nc.scalar.copy(out=w1_bf[:], in_=w1_raw[:].rearrange("p j w -> p w j"))
         w1_codes = sb.tile([P, R], U32, name="w1_codes", align_bytes=64)
         w1_scales = sb.tile([P, R], U8, name="w1_scales", align_bytes=64)
-
-        g_planes = [sb.tile([P, JH], U8, name="g_planes0", align_bytes=64)]
-        nc.vector.tensor_copy(g_planes[0][:], planes[:].indirect(offsets[:, : JH // 16]))
         nc.vector.quantize_mx(out=w1_codes[:].bitcast(FP8X4), scales=w1_scales[:], in_=w1_bf[:].rearrange("p w j -> p (w j)"))
-        g_planes.append(sb.tile([P, JH], U8, name="g_planes1", tag="w1_bf_then_old", align_bytes=64))
-        nc.vector.tensor_copy(g_planes[1][:], planes[:].indirect(offsets[:, JH // 16 :]))
+
+        g_planes = sb.tile([P, J], U8, name="g_planes", align_bytes=64)
+        nc.vector.tensor_copy(g_planes[:], planes[:].indirect(offsets[:]))
+        g_words = [sb.tile([P, JH], U16, name="g_words%d" % h, align_bytes=64) for h in range(HALVES)]
+        for h in range(HALVES):
+            nc.vector.tensor_copy(g_words[h][:], words[:].indirect(offsets[:, h * (JH // 16) : (h + 1) * (JH // 16)]))
 
         a = [ps.tile([P, JQ], F32, name="a%d" % q) for q in range(QUARTERS)]
         u = [
@@ -75,17 +73,19 @@ def tile_attend_cgeometricpool_kernel(tc, tab_words, tab_scales, w1, floor, wo, 
                 out=a[q][:],
                 lhsT=w1_codes[:].bitcast(FP8X4),
                 lhsT_scale=w1_scales[:],
-                rhs=g_words[:, quarter[q]].bitcast(FP4X4),
-                rhs_scale=g_planes[q // 2][:, (q % 2) * JQ : (q % 2 + 1) * JQ],
+                rhs=g_words[q // 2][:, quarter[q % 2]].bitcast(FP4X4),
+                rhs_scale=g_planes[:, quarter[q]],
                 start=True,
                 stop=True,
             )
             nc.scalar.activation(out=u[q // 2][:, quarter[q % 2]], in_=a[q][:], func=ACT.Tanh, scale=0.5)
 
-        wo_raw = sb.tile([P, PACK, R], F32, name="wo_raw", tag="weights_raw", align_bytes=64)
-        dy_raw = sb.tile([P, PACK, G], F32, name="dy_raw", tag="words_then_dy", align_bytes=64)
-        old_sb = sb.tile([P, J], F32, name="old_sb", tag="w1_bf_then_old", align_bytes=64)
+        wo_raw = sb.tile([P, PACK, R], F32, name="wo_raw", tag="w1_raw_then_wo", align_bytes=64)
+        floor_sb = sb.tile([P, 1], F32, name="floor_sb", tag="w1_bf_then_floor", align_bytes=64)
+        dy_raw = sb.tile([P, PACK, G], F32, name="dy_raw", tag="planes_then_dy", align_bytes=64)
+        old_sb = sb.tile([P, J], F32, name="old_sb", tag="words_then_old", align_bytes=64)
         nc.sync.dma_start(out=wo_raw[:], in_=wo.rearrange("(p j) w -> p j w", j=PACK))
+        nc.sync.dma_start(out=floor_sb[:], in_=floor)
         nc.sync.dma_start(out=dy_raw[:], in_=dy.rearrange("(p j) w -> p j w", j=PACK))
         nc.sync.dma_start(out=old_sb[:], in_=old)
 
@@ -125,16 +125,13 @@ def tile_attend_cgeometricpool_kernel(tc, tab_words, tab_scales, w1, floor, wo, 
             nc.scalar.activation(out=h1[:, cols], in_=h0[:, cols], func=ACT.Ln, bias=floor_sb[:], scale=1.0)
         for q, cols in enumerate(quarter):
             nc.vector.tensor_tensor(out=y[:, cols], in0=a[q][:], in1=h0[:, cols], op=ALU.subtract)
-        sums = sb.tile([P, G], F32, name="sums")
+        sums = sb.tile([P, G], F32, name="sums", tag="sums_then_w")
         z = sb.tile([P, J], F32, name="z")
-        for h in range(HALVES):
-            nc.vector.tensor_reduce(
-                out=sums[:, groups[h]], in_=h1[:, halves[h]].rearrange("p (g i) -> p g i", i=POOL), axis=AX.X, op=ALU.add
-            )
+        nc.vector.tensor_reduce(out=sums[:], in_=h1[:].rearrange("p (g i) -> p g i", i=POOL), axis=AX.X, op=ALU.add)
         for cols in halves:
             nc.vector.tensor_tensor(out=z[:, cols], in0=y[:, cols], in1=h1[:, cols], op=ALU.subtract)
 
-        gm = sb.tile([P, G], F32, name="gm", tag="gm_then_w")
+        gm = sb.tile([P, G], F32, name="gm")
         u1 = sb.tile([P, G], F32, name="tanh_gm")
         for grp in groups:
             nc.scalar.activation(out=gm[:, grp], in_=sums[:, grp], func=ACT.Exp, scale=1.0 / POOL)
@@ -145,7 +142,7 @@ def tile_attend_cgeometricpool_kernel(tc, tab_words, tab_scales, w1, floor, wo, 
         u2 = sb.tile([P, G], F32, name="u2")
         e1 = sb.tile([P, G], F32, name="e1")
         nc.vector.scalar_tensor_tensor(out=cg[:], in0=c0[:], scalar=-1.0 / POOL, in1=gm[:], op0=ALU.mult, op1=ALU.mult)
-        w = sb.tile([P, J], F32, name="w", tag="gm_then_w")
+        w = sb.tile([P, J], F32, name="w", tag="sums_then_w")
         for cols in halves:
             nc.scalar.activation(out=w[:, cols], in_=z[:, cols], func=ACT.Exp)
         for grp in groups:

from contextlib import ExitStack

import concourse.mybir as mybir

K, R, F, T, J, G = 512, 128, 512, 2048, 512, 128
FLOPS = 2 * K * R * J + 2 * F * R * G

F32 = mybir.dt.float32
BF16 = mybir.dt.bfloat16
I32 = mybir.dt.int32
U32 = mybir.dt.uint32
U16 = mybir.dt.uint16
U8 = mybir.dt.uint8
FP8X4 = mybir.dt.float8_e4m3fn_x4
FP4X4 = mybir.dt.float4_e2m1fn_x4
ACT = mybir.ActivationFunctionType
ALU = mybir.AluOpType
AX = mybir.AxisListType

P = 128
PACK = 4
POOL = J // G
HALVES = 2
JH = J // HALVES
GH = G // HALVES
QUARTERS = 4
JQ = J // QUARTERS


def tile_attend_cgeometricpool_kernel(tc, tab_words, tab_scales, w1, floor, wo, dy, old, offs, out):
    nc = tc.nc
    with ExitStack() as ctx:
        sb = ctx.enter_context(tc.tile_pool(name="sb", bufs=1))
        ps = ctx.enter_context(tc.psum_pool(name="ps", bufs=1))

        offsets = sb.tile([P, J // 16], U16, name="offsets")
        planes = sb.tile([P, T], U8, name="planes", tag="planes_then_dy", align_bytes=64)
        w1_raw = sb.tile([P, PACK, R], F32, name="w1_raw", tag="w1_raw_then_wo", align_bytes=64)
        one = sb.tile([P, 1], F32, name="one", tag="words_then_old", align_bytes=64)
        half = sb.tile([P, 1], F32, name="half")

        nc.vector.memset(one[:], 1.0)
        nc.vector.memset(planes[:].bitcast(I32), 0)
        nc.vector.tensor_scalar_mul(out=half[:], in0=one[:], scalar1=0.5)
        nc.sync.dma_start(out=w1_raw[:], in_=w1.rearrange("(p j) w -> p j w", j=PACK))
        nc.sync.dma_start(offsets[:], offs)
        for q in range(4):
            nc.sync.dma_start(out=planes[32 * q : 32 * q + 4, :].bitcast(I32), in_=tab_scales[0, 4 * q : 4 * q + 4, :].bitcast(I32))
        words = sb.tile([P, T], U16, name="words", tag="words_then_old", align_bytes=64)
        nc.sync.dma_start(out=words[:].bitcast(I32), in_=tab_words[0].bitcast(I32))

        w1_bf = sb.tile([P, R, PACK], BF16, name="w1_bf", tag="w1_bf_then_floor", align_bytes=64)
        nc.scalar.copy(out=w1_bf[:], in_=w1_raw[:].rearrange("p j w -> p w j"))
        w1_codes = sb.tile([P, R], U32, name="w1_codes", align_bytes=64)
        w1_scales = sb.tile([P, R], U8, name="w1_scales", align_bytes=64)
        nc.vector.quantize_mx(out=w1_codes[:].bitcast(FP8X4), scales=w1_scales[:], in_=w1_bf[:].rearrange("p w j -> p (w j)"))

        g_planes = sb.tile([P, J], U8, name="g_planes", align_bytes=64)
        nc.vector.tensor_copy(g_planes[:], planes[:].indirect(offsets[:]))
        g_words = [sb.tile([P, JH], U16, name="g_words%d" % h, align_bytes=64) for h in range(HALVES)]
        for h in range(HALVES):
            nc.vector.tensor_copy(g_words[h][:], words[:].indirect(offsets[:, h * (JH // 16) : (h + 1) * (JH // 16)]))

        a = [ps.tile([P, JQ], F32, name="a%d" % q) for q in range(QUARTERS)]
        u = [
            sb.tile([P, JH], F32, name="u0", tag="pair_then_h0", align_bytes=64),
            sb.tile([P, JH], F32, name="u1", align_bytes=64),
        ]
        absu = sb.tile([P, J], F32, name="absu")
        quarter = [slice(q * JQ, (q + 1) * JQ) for q in range(QUARTERS)]
        for q in range(QUARTERS):
            nc.tensor.matmul_mx(
                out=a[q][:],
                lhsT=w1_codes[:].bitcast(FP8X4),
                lhsT_scale=w1_scales[:],
                rhs=g_words[q // 2][:, quarter[q % 2]].bitcast(FP4X4),
                rhs_scale=g_planes[:, quarter[q]],
                start=True,
                stop=True,
            )
            nc.scalar.activation(out=u[q // 2][:, quarter[q % 2]], in_=a[q][:], func=ACT.Tanh, scale=0.5)

        wo_raw = sb.tile([P, PACK, R], F32, name="wo_raw", tag="w1_raw_then_wo", align_bytes=64)
        floor_sb = sb.tile([P, 1], F32, name="floor_sb", tag="w1_bf_then_floor", align_bytes=64)
        dy_raw = sb.tile([P, PACK, G], F32, name="dy_raw", tag="planes_then_dy", align_bytes=64)
        old_sb = sb.tile([P, J], F32, name="old_sb", tag="words_then_old", align_bytes=64)
        nc.sync.dma_start(out=wo_raw[:], in_=wo.rearrange("(p j) w -> p j w", j=PACK))
        nc.sync.dma_start(out=floor_sb[:], in_=floor)
        nc.sync.dma_start(out=dy_raw[:], in_=dy.rearrange("(p j) w -> p j w", j=PACK))
        nc.sync.dma_start(out=old_sb[:], in_=old)

        halves = [slice(h * JH, (h + 1) * JH) for h in range(HALVES)]
        groups = [slice(h * GH, (h + 1) * GH) for h in range(HALVES)]
        for h, cols in enumerate(halves):
            nc.vector.scalar_tensor_tensor(out=absu[:, cols], in0=u[h][:], scalar=-1.0, in1=u[h][:], op0=ALU.mult, op1=ALU.max)
        pair_bf = sb.tile([P, 2, R, PACK], BF16, name="pair_bf", tag="pair_then_h0", align_bytes=64)
        nc.vector.tensor_copy(out=pair_bf[:, 0], in_=wo_raw[:].rearrange("p j w -> p w j"))
        nc.vector.tensor_copy(out=pair_bf[:, 1], in_=dy_raw[:].rearrange("p j w -> p w j"))
        pair_codes = sb.tile([P, 2 * R], U32, name="pair_codes", align_bytes=64)
        pair_scales = sb.tile([P, 2 * R], U8, name="pair_scales", align_bytes=64)
        nc.vector.quantize_mx(
            out=pair_codes[:].bitcast(FP8X4), scales=pair_scales[:], in_=pair_bf[:].rearrange("p s w j -> p (s w j)")
        )
        c0 = ps.tile([P, G], F32, name="c0")
        nc.tensor.matmul_mx(
            out=c0[:],
            lhsT=pair_codes[:, :R].bitcast(FP8X4),
            lhsT_scale=pair_scales[:, :R],
            rhs=pair_codes[:, R:].bitcast(FP8X4),
            rhs_scale=pair_scales[:, R:],
            start=True,
            stop=True,
        )

        lsig = sb.tile([P, J], F32, name="lsig")
        for cols in quarter:
            nc.scalar.activation(out=lsig[:, cols], in_=absu[:, cols], func=ACT.Ln, bias=half[:], scale=0.5)

        h0 = sb.tile([P, J], F32, name="h0", tag="pair_then_h0", align_bytes=64)
        h1 = sb.tile([P, J], F32, name="h1")
        y = sb.tile([P, J], F32, name="y")
        for q, cols in enumerate(quarter):
            nc.vector.scalar_tensor_tensor(out=h0[:, cols], in0=a[q][:], scalar=0.0, in1=lsig[:, cols], op0=ALU.max, op1=ALU.subtract)
        for cols in quarter:
            nc.scalar.activation(out=h1[:, cols], in_=h0[:, cols], func=ACT.Ln, bias=floor_sb[:], scale=1.0)
        for q, cols in enumerate(quarter):
            nc.vector.tensor_tensor(out=y[:, cols], in0=a[q][:], in1=h0[:, cols], op=ALU.subtract)
        sums = sb.tile([P, G], F32, name="sums", tag="sums_then_w")
        z = sb.tile([P, J], F32, name="z")
        nc.vector.tensor_reduce(out=sums[:], in_=h1[:].rearrange("p (g i) -> p g i", i=POOL), axis=AX.X, op=ALU.add)
        for cols in halves:
            nc.vector.tensor_tensor(out=z[:, cols], in0=y[:, cols], in1=h1[:, cols], op=ALU.subtract)

        gm = sb.tile([P, G], F32, name="gm")
        u1 = sb.tile([P, G], F32, name="tanh_gm")
        for grp in groups:
            nc.scalar.activation(out=gm[:, grp], in_=sums[:, grp], func=ACT.Exp, scale=1.0 / POOL)
        for grp in groups:
            nc.scalar.activation(out=u1[:, grp], in_=gm[:, grp], func=ACT.Tanh)

        cg = sb.tile([P, G], F32, name="cg")
        u2 = sb.tile([P, G], F32, name="u2")
        e1 = sb.tile([P, G], F32, name="e1")
        nc.vector.scalar_tensor_tensor(out=cg[:], in0=c0[:], scalar=-1.0 / POOL, in1=gm[:], op0=ALU.mult, op1=ALU.mult)
        w = sb.tile([P, J], F32, name="w", tag="sums_then_w")
        for cols in halves:
            nc.scalar.activation(out=w[:, cols], in_=z[:, cols], func=ACT.Exp)
        for grp in groups:
            nc.vector.tensor_tensor(out=u2[:, grp], in0=u1[:, grp], in1=u1[:, grp], op=ALU.mult)
        for grp in groups:
            nc.vector.scalar_tensor_tensor(out=e1[:, grp], in0=u2[:, grp], scalar=1.0, in1=cg[:, grp], op0=ALU.subtract, op1=ALU.mult)

        da = sb.tile([P, G, POOL], F32, name="da")
        res = sb.tile([P, J], F32, name="res")
        for h in range(HALVES):
            nc.vector.tensor_tensor(
                out=da[:, groups[h], :],
                in0=w[:, halves[h]].rearrange("p (g i) -> p g i", i=POOL),
                in1=e1[:, groups[h]].unsqueeze(2).to_broadcast([P, GH, POOL]),
                op=ALU.mult,
            )
        for h in range(HALVES):
            cols = halves[h]
            nc.vector.tensor_tensor(
                out=res[:, cols], in0=da[:, groups[h], :].rearrange("p g i -> p (g i)"), in1=old_sb[:, cols], op=ALU.add
            )
            queue = nc.sync if h == 0 else nc.scalar
            queue.dma_start(out=out[:, cols], in_=res[:, cols])
